import numpy as np
import ml_dtypes


def mxq(x, axis, fmt="e4m3"):
    dtype, down = {"e4m3": (ml_dtypes.float8_e4m3fn, 7), "e5m2": (ml_dtypes.float8_e5m2, 14)}[fmt]
    v = np.moveaxis(np.asarray(x, np.float32).astype(ml_dtypes.bfloat16).astype(np.float64), axis, -1)
    blocks = v.reshape(v.shape[:-1] + (-1, 32))
    amax = np.abs(blocks).max(-1, keepdims=True)
    byte = np.maximum(np.where(amax > 0, np.frexp(amax)[1] - 1 + 127, 0) - down, 1)
    scale = np.exp2(byte - 127.0)
    codes = (blocks / scale).astype(np.float32).astype(dtype).astype(np.float64)
    return np.moveaxis((codes * scale).reshape(v.shape), -1, axis)


WIDE = False


def mx_kscale(k):
    if not WIDE:
        return np.ones(k)
    levels = np.array([10, -10, 5, -5, 0])
    if k % 512:
        return np.exp2(np.random.permutation(np.resize(levels, k // 32))).repeat(32)
    a = np.empty((k // 512, 16))
    for p in range(k // 512):
        a[p, :8] = np.random.permutation(np.resize(levels, 8))
        for g in range(8):
            far = levels[np.abs(levels - a[p, g]) >= 10]
            a[p, g + 8] = far[np.random.randint(len(far))]
    return np.exp2(a.ravel()).repeat(32)


def f64(x):
    return np.asarray(x).astype(np.float64)


def striped(idx):
    return np.tile(np.asarray(idx).reshape(-1, 16).T, (8, 1)).astype(np.uint16)


def unstriped(offs):
    return offs[:16].T.reshape(-1).astype(np.int64)


E2M1 = np.array([0.0, 0.5, 1.0, 1.5, 2.0, 3.0, 4.0, 6.0, -0.0, -0.5, -1.0, -1.5, -2.0, -3.0, -4.0, -6.0])


def pack_weight(w, fmt):
    k, n = w.shape
    w = f64(np.asarray(w, np.float32).astype(ml_dtypes.bfloat16)).reshape(k // 32, 32, n)
    amax = np.abs(w).max(1)
    if fmt == "e4m3":
        byte = np.frexp(amax)[1] - 1 + 127 - 7
    else:
        mant, ex = np.frexp(amax / 6.0)
        byte = np.where(mant > 0.5, ex, ex - 1) + 127
    byte = np.clip(np.where(amax > 0, byte, 1), 1, 254)
    scaled = (w * np.exp2(127.0 - byte)[:, None, :]).reshape(k, n).astype(np.float32)
    by_word = np.ascontiguousarray(scaled.reshape(k // 512, 128, 4, n).transpose(0, 1, 3, 2))
    if fmt == "e4m3":
        words = by_word.astype(ml_dtypes.float8_e4m3fn).view(np.uint8)
    else:
        c = by_word.astype(ml_dtypes.float4_e2m1fn).view(np.uint8) & 0xF
        words = (c[..., 0::2] | (c[..., 1::2] << 4)).reshape(k // 512, 128, 2 * n)
    return np.ascontiguousarray(words), np.ascontiguousarray(byte.astype(np.uint8).reshape(k // 512, 16, n))


def unpack_weight(words, scales, fmt):
    g, _, n = scales.shape
    words = np.ascontiguousarray(words).reshape(g, 128, n, -1)
    if fmt == "e4m3":
        vals = words.view(ml_dtypes.float8_e4m3fn).astype(np.float64)
    else:
        nib = np.empty((g, 128, n, 4), np.uint8)
        nib[..., 0::2] = words & 0xF
        nib[..., 1::2] = words >> 4
        vals = E2M1[nib]
    vals = vals * np.repeat(np.exp2(scales.astype(np.float64) - 127.0), 8, axis=1)[..., None]
    return vals.transpose(0, 1, 3, 2).reshape(g * 512, n)


B, N, T, D, DV, NQ = 1, 512, 2048, 1024, 256, 128


def setup_inputs():
    n = np.random.standard_normal
    idx = np.sort(np.random.permutation(T)[:B * N].reshape(B, N), axis=1).reshape(-1)
    s = mx_kscale(D)[:, None]
    u = np.ones(T)
    u[idx] = mx_kscale(B * N)
    r = np.random.uniform(0.5, 2.0, T)
    k = n((D, T)) / s
    v = n((DV, T)) / (u * r)
    kp = pack_weight(k, "e2m1")
    return {
        "qT": (n((B, D, NQ)) * s * (0.80 / np.sqrt(D))).astype(np.float32),
        "k_words": np.ascontiguousarray(kp[0].reshape(D // 1024, 2, 128, T, 2).transpose(0, 2, 3, 1, 4)).reshape(D // 1024, 128, T, 4),
        "k_scales": kp[1],
        "vT": v.astype(np.float32),
        "vs": np.tile(u * r, (128, 1)).astype(np.float32),
        "offs": striped(idx),
    }


def reference(qT, k_words, k_scales, vT, vs, offs):
    idx = unstriped(offs)
    k = unpack_weight(k_words.reshape(D // 1024, 128, T, 2, 2).transpose(0, 3, 1, 2, 4).reshape(D // 512, 128, 2 * T), k_scales, "e2m1")
    v = f64(vT)
    pick = lambda x: x[:, idx].reshape(x.shape[0], B, N).transpose(1, 0, 2)
    q = f64(qT)
    score = mxq(q, 1, "e4m3").transpose(0, 2, 1) @ pick(k)
    p = np.square(np.maximum(score, 0.0))
    total = p.sum(-1, keepdims=True) + 1.0
    w = p * pick(f64(vs))[:, :1, :]
    y = mxq(w, 2, "e4m3") @ mxq(pick(v).transpose(0, 2, 1), 1, "e4m3")
    y = y / total
    return y

@@ -1,0 +1,149 @@
+from contextlib import ExitStack
+
+import concourse.mybir as mybir
+from concourse.masks import make_identity
+
+F32 = mybir.dt.float32
+BF16 = mybir.dt.bfloat16
+I32 = mybir.dt.int32
+U32 = mybir.dt.uint32
+U16 = mybir.dt.uint16
+U8 = mybir.dt.uint8
+FP8X4 = mybir.dt.float8_e4m3fn_x4
+FP4X4 = mybir.dt.float4_e2m1fn_x4
+ACT = mybir.ActivationFunctionType
+ALU = mybir.AluOpType
+
+P = 128
+PACK = 4
+SLOTS, POOL, D, DV, NQ = 512, 2048, 1024, 256, 128
+PASSES = D // (P * PACK)
+PLANES = DV // P
+VS_ROW = P - 1
+
+FLOPS = 2 * NQ * SLOTS * (D + DV)
+BYTES = 4 * D * NQ + 4 * P * POOL + 32 * POOL + 4 * DV * POOL + 4 * POOL + 2 * SLOTS + 4 * NQ * DV
+
+
+def tile_attend_relu2_srt_kernel(tc, qT, k_words, k_scales, vT, vs, offs, out):
+    nc = tc.nc
+    with ExitStack() as ctx:
+        sb = ctx.enter_context(tc.tile_pool(name="sb", bufs=1))
+        lay = ctx.enter_context(tc.tile_pool(name="lay", bufs=1))
+        ps = ctx.enter_context(tc.psum_pool(name="ps", bufs=1))
+
+        offsets = sb.tile([P, SLOTS // 16], U16, name="offsets")
+        kw_pool = lay.tile([P, POOL], I32, name="kw_pool", offset=0)
+        ks_pool = lay.tile([P, POOL], U8, name="ks_pool", offset=17408)
+        vs_pool = lay.tile([P, POOL], F32, name="vs_pool", offset=8192)
+        v_pool = [lay.tile([P, POOL], F32, name=f"v_pool{j}", offset=(8192, 0)[j]) for j in range(PLANES)]
+        q_raw = sb.tile([P, PASSES, PACK, NQ], F32, name="q_raw")
+        one_set = sb.tile([P, 1], F32, name="one_set")
+        one = sb.tile([P, 1], F32, name="one")
+        ident = sb.tile([P, P], F32, name="ident")
+
+        ks = [sb.tile([P, SLOTS], U8, name=f"ks{o}", align_bytes=64) for o in range(PASSES)]
+        nc.vector.memset(ks_pool[:].bitcast(I32), 0)
+        nc.vector.memset(one_set[:], 1.0)
+        nc.vector.memset(vs_pool[0:VS_ROW, :].bitcast(I32), 0)
+        nc.vector.memset(ks[1][:].bitcast(I32), 0)
+        make_identity(nc, ident[:])
+
+        nc.sync.dma_start(offsets[:], offs)
+        nc.sync.dma_start(kw_pool[:], k_words[0].rearrange("p t b -> p (t b)").bitcast(I32))
+        nc.scalar.dma_start(vs_pool[VS_ROW:P, :], vs[0:1, :])
+        for quad in range(4):
+            nc.scalar.dma_start(
+                ks_pool[32 * quad : 32 * quad + 8, :].bitcast(I32),
+                k_scales[:, 4 * quad : 4 * quad + 4, :].bitcast(I32),
+            )
+        nc.scalar.copy(one[:], one_set[:])
+        nc.sync.dma_start(q_raw[:], qT[0].rearrange("(o p j) q -> p o j q", p=P, j=PACK))
+
+        vs_listed = sb.tile([P, SLOTS], F32, name="vs_listed")
+        nc.vector.tensor_copy(vs_listed[:], vs_pool[:].indirect(offsets[:]))
+        nc.sync.dma_start(v_pool[0][:], vT[0:P, :])
+        vs_turned = ps.tile([P, PACK, P], F32, name="vs_turned", offset=4096)
+        for t in range(PACK):
+            nc.tensor.transpose(vs_turned[:, t, :], vs_listed[:, t:SLOTS:PACK], ident[:])
+        vs_cols = sb.tile([P, PACK], F32, name="vs_cols")
+        nc.scalar.copy(vs_cols[:], vs_turned[:, :, VS_ROW])
+
+        nc.vector.tensor_copy(ks[0][:], ks_pool[:].indirect(offsets[:]))
+        nc.scalar.dma_start(ks[1][0:112, :].bitcast(I32), ks[0][4:116, :].bitcast(I32))
+        kw_pairs = lay.tile([P, SLOTS], U32, name="kw_pairs", offset=16384)
+        nc.vector.tensor_copy(kw_pairs[:], kw_pool[:].bitcast(U32).indirect(offsets[:]))
+        nc.sync.dma_start(v_pool[1][:], vT[P : 2 * P, :])
+        kw = [sb.tile([P, 2 * SLOTS], U8, name=f"kw{o}", align_bytes=64) for o in range(PASSES)]
+        halves = kw_pairs[:].bitcast(U16).rearrange("p (s h) -> p h s", h=2)
+        for o in range(PASSES):
+            nc.vector.tensor_copy(kw[o][:].bitcast(U16), halves[:, o, :])
+
+        q_bf = lay.tile([P, PASSES, NQ, PACK], BF16, name="q_bf", align_bytes=64, offset=18432)
+        nc.scalar.copy(q_bf[:], q_raw[:].rearrange("p o j q -> p o q j"))
+        q_codes = sb.tile([P, PASSES * NQ], U32, name="q_codes", align_bytes=64)
+        q_scales = sb.tile([P, PASSES * NQ], U8, name="q_scales", align_bytes=64)
+        nc.vector.quantize_mx(out=q_codes[:].bitcast(FP8X4), scales=q_scales[:], in_=q_bf[:].rearrange("p o q j -> p (o q j)"))
+
+        scores = ps.tile([P, SLOTS], F32, name="scores", offset=0)
+        for o in range(PASSES):
+            cols = slice(o * NQ, (o + 1) * NQ)
+            nc.tensor.matmul_mx(
+                out=scores[:],
+                lhsT=q_codes[:, cols].bitcast(FP8X4),
+                lhsT_scale=q_scales[:, cols],
+                rhs=kw[o][:].bitcast(FP4X4),
+                rhs_scale=ks[o][:],
+                start=(o == 0),
+                stop=(o == PASSES - 1),
+            )
+
+        pos = sb.tile([P, PACK, P], F32, name="pos")
+        nc.scalar.activation(pos[:], scores[:].rearrange("q (s t) -> q t s", t=PACK), ACT.Relu)
+        prob = lay.tile([P, PACK, P], F32, name="prob", offset=32768)
+        total = sb.tile([P, 1], F32, name="total")
+        nc.scalar.activation(prob[:], pos[:], ACT.Square, accum_out=total[:])
+        prob_turned = ps.tile([P, PACK, NQ], F32, name="prob_turned", offset=2048)
+        for t in range(PACK):
+            nc.tensor.transpose(prob_turned[:, t, :], prob[:, t, :], ident[:])
+        w_bf = sb.tile([P, NQ, PACK], BF16, name="w_bf", align_bytes=64)
+        nc.vector.tensor_tensor(
+            w_bf[:],
+            prob_turned[:].rearrange("p t q -> p q t"),
+            vs_cols[:].unsqueeze(1).to_broadcast([P, NQ, PACK]),
+            ALU.mult,
+        )
+        w_codes = sb.tile([P, NQ], U32, name="w_codes", align_bytes=64)
+        w_scales = sb.tile([P, NQ], U8, name="w_scales", align_bytes=64)
+        nc.vector.quantize_mx(out=w_codes[:].bitcast(FP8X4), scales=w_scales[:], in_=w_bf[:].rearrange("p q t -> p (q t)"))
+
+        denom = sb.tile([P, 1], F32, name="denom")
+        nc.scalar.activation(denom[:], total[:], ACT.Identity, bias=one[:])
+        inv = sb.tile([P, 1], F32, name="inv")
+        nc.vector.reciprocal(inv[:], denom[:])
+
+        for j in range(PLANES):
+            v_listed = lay.tile([P, SLOTS], BF16, name=f"v_listed{j}", offset=(18432, 32768)[j])
+            nc.vector.tensor_copy(v_listed[:], v_pool[j][:].indirect(offsets[:]))
+            v_words = v_listed[:].bitcast(F32)
+            v_turned = ps.tile([P, 2, P], F32, name=f"v_turned{j}", offset=2048 * j)
+            for u in range(2):
+                nc.tensor.transpose(v_turned[:, u, :], v_words[:, u : SLOTS // 2 : 2], ident[:])
+            v_bf = sb.tile([P, P * PACK], BF16, name=f"v_bf{j}", align_bytes=64)
+            nc.scalar.copy(v_bf[:].bitcast(F32).rearrange("p (e u) -> p e u", u=2), v_turned[:].rearrange("p u e -> p e u"))
+            v_codes = sb.tile([P, P], U32, name=f"v_codes{j}", align_bytes=64)
+            v_scales = sb.tile([P, P], U8, name=f"v_scales{j}", align_bytes=64)
+            nc.vector.quantize_mx(out=v_codes[:].bitcast(FP8X4), scales=v_scales[:], in_=v_bf[:])
+            sums = ps.tile([P, P], F32, name=f"sums{j}", offset=6144 + 2048 * j)
+            nc.tensor.matmul_mx(
+                out=sums[:],
+                lhsT=w_codes[:].bitcast(FP8X4),
+                lhsT_scale=w_scales[:],
+                rhs=v_codes[:].bitcast(FP8X4),
+                rhs_scale=v_scales[:],
+                start=True,
+                stop=True,
+            )
+            y = sb.tile([P, P], F32, name=f"y{j}")
+            nc.scalar.activation(y[:], sums[:], ACT.Copy, scale=inv[:])
+            nc.sync.dma_start(out[0][:, j * P : (j + 1) * P], y[:])

@@ -33,59 +33,61 @@ def tile_attend_relu2_srt_kernel(tc, qT, k_words, k_scales, vT, vs, offs, out):
         ps = ctx.enter_context(tc.psum_pool(name="ps", bufs=1))
 
         offsets = sb.tile([P, SLOTS // 16], U16, name="offsets")
-        kw_pool = lay.tile([P, POOL], I32, name="kw_pool", offset=0)
-        ks_pool = lay.tile([P, POOL], U8, name="ks_pool", offset=17408)
-        vs_pool = lay.tile([P, POOL], F32, name="vs_pool", offset=8192)
-        v_pool = [lay.tile([P, POOL], F32, name=f"v_pool{j}", offset=(8192, 0)[j]) for j in range(PLANES)]
-        q_raw = sb.tile([P, PASSES, PACK, NQ], F32, name="q_raw")
-        one_set = sb.tile([P, 1], F32, name="one_set")
-        one = sb.tile([P, 1], F32, name="one")
+        kw_pool = sb.tile([P, POOL], I32, name="kw_pool")
+        ks_pool = sb.tile([P, PASSES, POOL], U8, name="ks_pool")
+        vs_pool = lay.tile([P, POOL], F32, name="vs_pool", offset=12288)
+        one_set = lay.tile([P, 16], F32, name="one_set", offset=4096 - 32)
+        q_raw = lay.tile([P, PASSES, PACK, NQ], F32, name="q_raw", offset=0)
+        v_pool = [lay.tile([P, POOL], F32, name=f"v_pool{j}", offset=(4096, 12288)[j]) for j in range(PLANES)]
+        one = sb.tile([P, 16], F32, name="one")
         ident = sb.tile([P, P], F32, name="ident")
 
-        ks = [sb.tile([P, SLOTS], U8, name=f"ks{o}", align_bytes=64) for o in range(PASSES)]
-        nc.vector.memset(ks_pool[:].bitcast(I32), 0)
+        nc.vector.memset(ks_pool[:].rearrange("p o t -> p (o t)").bitcast(I32), 0)
         nc.vector.memset(one_set[:], 1.0)
         nc.vector.memset(vs_pool[0:VS_ROW, :].bitcast(I32), 0)
-        nc.vector.memset(ks[1][:].bitcast(I32), 0)
         make_identity(nc, ident[:])
 
         nc.sync.dma_start(offsets[:], offs)
+        nc.sync.dma_start(vs_pool[VS_ROW:P, :], vs[0:1, :])
         nc.sync.dma_start(kw_pool[:], k_words[0].rearrange("p t b -> p (t b)").bitcast(I32))
-        nc.scalar.dma_start(vs_pool[VS_ROW:P, :], vs[0:1, :])
         for quad in range(4):
-            nc.scalar.dma_start(
-                ks_pool[32 * quad : 32 * quad + 8, :].bitcast(I32),
-                k_scales[:, 4 * quad : 4 * quad + 4, :].bitcast(I32),
+            nc.sync.dma_start(
+                ks_pool[32 * quad : 32 * quad + 4, :, :].bitcast(I32),
+                k_scales[:, 4 * quad : 4 * quad + 4, :].rearrange("o r t -> r o t").bitcast(I32),
             )
         nc.scalar.copy(one[:], one_set[:])
         nc.sync.dma_start(q_raw[:], qT[0].rearrange("(o p j) q -> p o j q", p=P, j=PACK))
+        nc.sync.dma_start(v_pool[0][:], vT[0:P, :])
 
         vs_listed = sb.tile([P, SLOTS], F32, name="vs_listed")
         nc.vector.tensor_copy(vs_listed[:], vs_pool[:].indirect(offsets[:]))
-        nc.sync.dma_start(v_pool[0][:], vT[0:P, :])
-        vs_turned = ps.tile([P, PACK, P], F32, name="vs_turned", offset=4096)
+        nc.sync.dma_start(v_pool[1][:], vT[P : 2 * P, :])
+        vs_turned = ps.tile([P, PACK, P], F32, name="vs_turned")
         for t in range(PACK):
             nc.tensor.transpose(vs_turned[:, t, :], vs_listed[:, t:SLOTS:PACK], ident[:])
         vs_cols = sb.tile([P, PACK], F32, name="vs_cols")
         nc.scalar.copy(vs_cols[:], vs_turned[:, :, VS_ROW])
 
-        nc.vector.tensor_copy(ks[0][:], ks_pool[:].indirect(offsets[:]))
-        nc.scalar.dma_start(ks[1][0:112, :].bitcast(I32), ks[0][4:116, :].bitcast(I32))
-        kw_pairs = lay.tile([P, SLOTS], U32, name="kw_pairs", offset=16384)
+        kw_pairs = sb.tile([P, SLOTS], U32, name="kw_pairs")
         nc.vector.tensor_copy(kw_pairs[:], kw_pool[:].bitcast(U32).indirect(offsets[:]))
-        nc.sync.dma_start(v_pool[1][:], vT[P : 2 * P, :])
+        ks0 = sb.tile([P, SLOTS], U8, name="ks0", align_bytes=64)
+        nc.vector.tensor_copy(ks0[:], ks_pool[:, 0, :].indirect(offsets[:]))
         kw = [sb.tile([P, 2 * SLOTS], U8, name=f"kw{o}", align_bytes=64) for o in range(PASSES)]
         halves = kw_pairs[:].bitcast(U16).rearrange("p (s h) -> p h s", h=2)
         for o in range(PASSES):
             nc.vector.tensor_copy(kw[o][:].bitcast(U16), halves[:, o, :])
 
-        q_bf = lay.tile([P, PASSES, NQ, PACK], BF16, name="q_bf", align_bytes=64, offset=18432)
+        q_bf = lay.tile([P, PASSES, NQ, PACK], BF16, name="q_bf", align_bytes=64, offset=20480)
         nc.scalar.copy(q_bf[:], q_raw[:].rearrange("p o j q -> p o q j"))
         q_codes = sb.tile([P, PASSES * NQ], U32, name="q_codes", align_bytes=64)
         q_scales = sb.tile([P, PASSES * NQ], U8, name="q_scales", align_bytes=64)
         nc.vector.quantize_mx(out=q_codes[:].bitcast(FP8X4), scales=q_scales[:], in_=q_bf[:].rearrange("p o q j -> p (o q j)"))
 
-        scores = ps.tile([P, SLOTS], F32, name="scores", offset=0)
+        ks1 = lay.tile([P, SLOTS], U8, name="ks1", align_bytes=64, offset=20480)
+        nc.vector.tensor_copy(ks1[:], ks_pool[:, 1, :].indirect(offsets[:]))
+        ks = [ks0, ks1]
+
+        scores = ps.tile([P, SLOTS], F32, name="scores")
         for o in range(PASSES):
             cols = slice(o * NQ, (o + 1) * NQ)
             nc.tensor.matmul_mx(
@@ -98,12 +100,12 @@ def tile_attend_relu2_srt_kernel(tc, qT, k_words, k_scales, vT, vs, offs, out):
                 stop=(o == PASSES - 1),
             )
 
-        pos = sb.tile([P, PACK, P], F32, name="pos")
+        pos = lay.tile([P, PACK, P], F32, name="pos", offset=22528)
         nc.scalar.activation(pos[:], scores[:].rearrange("q (s t) -> q t s", t=PACK), ACT.Relu)
-        prob = lay.tile([P, PACK, P], F32, name="prob", offset=32768)
+        prob = sb.tile([P, PACK, P], F32, name="prob")
         total = sb.tile([P, 1], F32, name="total")
         nc.scalar.activation(prob[:], pos[:], ACT.Square, accum_out=total[:])
-        prob_turned = ps.tile([P, PACK, NQ], F32, name="prob_turned", offset=2048)
+        prob_turned = ps.tile([P, PACK, NQ], F32, name="prob_turned")
         for t in range(PACK):
             nc.tensor.transpose(prob_turned[:, t, :], prob[:, t, :], ident[:])
         w_bf = sb.tile([P, NQ, PACK], BF16, name="w_bf", align_bytes=64)
@@ -118,15 +120,15 @@ def tile_attend_relu2_srt_kernel(tc, qT, k_words, k_scales, vT, vs, offs, out):
         nc.vector.quantize_mx(out=w_codes[:].bitcast(FP8X4), scales=w_scales[:], in_=w_bf[:].rearrange("p q t -> p (q t)"))
 
         denom = sb.tile([P, 1], F32, name="denom")
-        nc.scalar.activation(denom[:], total[:], ACT.Identity, bias=one[:])
+        nc.scalar.activation(denom[:], total[:], ACT.Identity, bias=one[:, 0:1])
         inv = sb.tile([P, 1], F32, name="inv")
         nc.vector.reciprocal(inv[:], denom[:])
 
         for j in range(PLANES):
-            v_listed = lay.tile([P, SLOTS], BF16, name=f"v_listed{j}", offset=(18432, 32768)[j])
+            v_listed = lay.tile([P, SLOTS], BF16, name=f"v_listed{j}", offset=(21504, 22528)[j])
             nc.vector.tensor_copy(v_listed[:], v_pool[j][:].indirect(offsets[:]))
             v_words = v_listed[:].bitcast(F32)
-            v_turned = ps.tile([P, 2, P], F32, name=f"v_turned{j}", offset=2048 * j)
+            v_turned = ps.tile([P, 2, P], F32, name=f"v_turned{j}")
             for u in range(2):
                 nc.tensor.transpose(v_turned[:, u, :], v_words[:, u : SLOTS // 2 : 2], ident[:])
             v_bf = sb.tile([P, P * PACK], BF16, name=f"v_bf{j}", align_bytes=64)
@@ -134,7 +136,7 @@ def tile_attend_relu2_srt_kernel(tc, qT, k_words, k_scales, vT, vs, offs, out):
             v_codes = sb.tile([P, P], U32, name=f"v_codes{j}", align_bytes=64)
             v_scales = sb.tile([P, P], U8, name=f"v_scales{j}", align_bytes=64)
             nc.vector.quantize_mx(out=v_codes[:].bitcast(FP8X4), scales=v_scales[:], in_=v_bf[:])
-            sums = ps.tile([P, P], F32, name=f"sums{j}", offset=6144 + 2048 * j)
+            sums = ps.tile([P, P], F32, name=f"sums{j}")
             nc.tensor.matmul_mx(
                 out=sums[:],
                 lhsT=w_codes[:].bitcast(FP8X4),

@@ -44,7 +44,8 @@ def tile_attend_relu2_srt_kernel(tc, qT, k_words, k_scales, vT, vs, offs, out):
 
         nc.vector.memset(ks_pool[:].rearrange("p o t -> p (o t)").bitcast(I32), 0)
         nc.vector.memset(one_set[:], 1.0)
-        nc.vector.memset(vs_pool[0:VS_ROW, :].bitcast(I32), 0)
+        nc.vector.memset(vs_pool[0:VS_ROW, POOL // 2 :].bitcast(I32), 0)
+        nc.gpsimd.memset(vs_pool[0:VS_ROW, : POOL // 2].bitcast(I32), 0)
         make_identity(nc, ident[:])
 
         nc.sync.dma_start(offsets[:], offs)
@@ -100,30 +101,19 @@ def tile_attend_relu2_srt_kernel(tc, qT, k_words, k_scales, vT, vs, offs, out):
                 stop=(o == PASSES - 1),
             )
 
-        pos = lay.tile([P, PACK, P], F32, name="pos", offset=22528)
-        nc.scalar.activation(pos[:], scores[:].rearrange("q (s t) -> q t s", t=PACK), ACT.Relu)
+        pos = sb.tile([P, PACK, P], F32, name="pos")
         prob = sb.tile([P, PACK, P], F32, name="prob")
-        total = sb.tile([P, 1], F32, name="total")
-        nc.scalar.activation(prob[:], pos[:], ACT.Square, accum_out=total[:])
+        total = sb.tile([P, 2], F32, name="total")
         prob_turned = ps.tile([P, PACK, NQ], F32, name="prob_turned")
-        for t in range(PACK):
-            nc.tensor.transpose(prob_turned[:, t, :], prob[:, t, :], ident[:])
-        w_bf = sb.tile([P, NQ, PACK], BF16, name="w_bf", align_bytes=64)
-        nc.vector.tensor_tensor(
-            w_bf[:],
-            prob_turned[:].rearrange("p t q -> p q t"),
-            vs_cols[:].unsqueeze(1).to_broadcast([P, NQ, PACK]),
-            ALU.mult,
-        )
-        w_codes = sb.tile([P, NQ], U32, name="w_codes", align_bytes=64)
-        w_scales = sb.tile([P, NQ], U8, name="w_scales", align_bytes=64)
-        nc.vector.quantize_mx(out=w_codes[:].bitcast(FP8X4), scales=w_scales[:], in_=w_bf[:].rearrange("p q t -> p (q t)"))
+        dealt = scores[:].rearrange("q (s t) -> q t s", t=PACK)
+        for half in range(2):
+            places = slice(2 * half, 2 * half + 2)
+            nc.scalar.activation(pos[:, places, :], dealt[:, places, :], ACT.Relu)
+            nc.scalar.activation(prob[:, places, :], pos[:, places, :], ACT.Square, accum_out=total[:, half : half + 1])
+            for t in range(2 * half, 2 * half + 2):
+                nc.tensor.transpose(prob_turned[:, t, :], prob[:, t, :], ident[:])
 
-        denom = sb.tile([P, 1], F32, name="denom")
-        nc.scalar.activation(denom[:], total[:], ACT.Identity, bias=one[:, 0:1])
-        inv = sb.tile([P, 1], F32, name="inv")
-        nc.vector.reciprocal(inv[:], denom[:])
-
+        v_bf = []
         for j in range(PLANES):
             v_listed = lay.tile([P, SLOTS], BF16, name=f"v_listed{j}", offset=(21504, 22528)[j])
             nc.vector.tensor_copy(v_listed[:], v_pool[j][:].indirect(offsets[:]))
@@ -131,18 +121,40 @@ def tile_attend_relu2_srt_kernel(tc, qT, k_words, k_scales, vT, vs, offs, out):
             v_turned = ps.tile([P, 2, P], F32, name=f"v_turned{j}")
             for u in range(2):
                 nc.tensor.transpose(v_turned[:, u, :], v_words[:, u : SLOTS // 2 : 2], ident[:])
-            v_bf = sb.tile([P, P * PACK], BF16, name=f"v_bf{j}", align_bytes=64)
-            nc.scalar.copy(v_bf[:].bitcast(F32).rearrange("p (e u) -> p e u", u=2), v_turned[:].rearrange("p u e -> p e u"))
-            v_codes = sb.tile([P, P], U32, name=f"v_codes{j}", align_bytes=64)
-            v_scales = sb.tile([P, P], U8, name=f"v_scales{j}", align_bytes=64)
-            nc.vector.quantize_mx(out=v_codes[:].bitcast(FP8X4), scales=v_scales[:], in_=v_bf[:])
+            v_bf.append(sb.tile([P, P * PACK], BF16, name=f"v_bf{j}", align_bytes=64))
+            nc.scalar.copy(v_bf[j][:].bitcast(F32).rearrange("p (e u) -> p e u", u=2), v_turned[:].rearrange("p u e -> p e u"))
+
+        w_bf = lay.tile([P, NQ, PACK], BF16, name="w_bf", align_bytes=64, offset=12288)
+        nc.vector.tensor_tensor(
+            w_bf[:],
+            prob_turned[:].rearrange("p t q -> p q t"),
+            vs_cols[:].unsqueeze(1).to_broadcast([P, NQ, PACK]),
+            ALU.mult,
+        )
+        v_codes = [lay.tile([P, P], U32, name=f"v_codes{j}", align_bytes=64, offset=12288 + 1024 + 512 * j) for j in range(PLANES)]
+        v_scales = [sb.tile([P, P], U8, name=f"v_scales{j}", align_bytes=64) for j in range(PLANES)]
+        nc.vector.quantize_mx(out=v_codes[0][:].bitcast(FP8X4), scales=v_scales[0][:], in_=v_bf[0][:])
+        w_codes = sb.tile([P, NQ], U32, name="w_codes", align_bytes=64)
+        w_scales = sb.tile([P, NQ], U8, name="w_scales", align_bytes=64)
+        nc.vector.quantize_mx(out=w_codes[:].bitcast(FP8X4), scales=w_scales[:], in_=w_bf[:].rearrange("p q t -> p (q t)"))
+
+        denom = sb.tile([P, 1], F32, name="denom")
+        part = sb.tile([P, 1], F32, name="part")
+        nc.scalar.activation(part[:], total[:, 0:1], ACT.Identity, bias=one[:, 0:1])
+        nc.scalar.activation(denom[:], total[:, 1:2], ACT.Identity, bias=part[:])
+        inv = lay.tile([P, 1], F32, name="inv", offset=12288 + 2048)
+        nc.vector.reciprocal(inv[:], denom[:])
+
+        nc.vector.quantize_mx(out=v_codes[1][:].bitcast(FP8X4), scales=v_scales[1][:], in_=v_bf[1][:])
+
+        for j in range(PLANES):
             sums = ps.tile([P, P], F32, name=f"sums{j}")
             nc.tensor.matmul_mx(
                 out=sums[:],
                 lhsT=w_codes[:].bitcast(FP8X4),
                 lhsT_scale=w_scales[:],
-                rhs=v_codes[:].bitcast(FP8X4),
-                rhs_scale=v_scales[:],
+                rhs=v_codes[j][:].bitcast(FP8X4),
+                rhs_scale=v_scales[j][:],
                 start=True,
                 stop=True,
             )

@@ -49,12 +49,12 @@ def tile_attend_relu2_srt_kernel(tc, qT, k_words, k_scales, vT, vs, offs, out):
         make_identity(nc, ident[:])
 
         nc.sync.dma_start(offsets[:], offs)
-        nc.sync.dma_start(vs_pool[VS_ROW:P, :], vs[0:1, :])
+        nc.scalar.dma_start(vs_pool[VS_ROW:P, :], vs[0:1, :])
         nc.sync.dma_start(kw_pool[:], k_words[0].rearrange("p t b -> p (t b)").bitcast(I32))
-        for quad in range(4):
+        for r in range(4):
             nc.sync.dma_start(
-                ks_pool[32 * quad : 32 * quad + 4, :, :].bitcast(I32),
-                k_scales[:, 4 * quad : 4 * quad + 4, :].rearrange("o r t -> r o t").bitcast(I32),
+                ks_pool[r:P:32, :, :].bitcast(I32),
+                k_scales[:, r:16:4, :].rearrange("o quad t -> quad o t").bitcast(I32),
             )
         nc.scalar.copy(one[:], one_set[:])
         nc.sync.dma_start(q_raw[:], qT[0].rearrange("(o p j) q -> p o j q", p=P, j=PACK))

@@ -44,6 +44,7 @@ def tile_attend_relu2_srt_kernel(tc, qT, k_words, k_scales, vT, vs, offs, out):
 
         nc.vector.memset(ks_pool[:].rearrange("p o t -> p (o t)").bitcast(I32), 0)
         nc.vector.memset(one_set[:], 1.0)
+        nc.vector.tensor_copy(one[:], one_set[:])
         nc.vector.memset(vs_pool[0:VS_ROW, POOL // 2 :].bitcast(I32), 0)
         nc.gpsimd.memset(vs_pool[0:VS_ROW, : POOL // 2].bitcast(I32), 0)
         make_identity(nc, ident[:])
@@ -56,7 +57,6 @@ def tile_attend_relu2_srt_kernel(tc, qT, k_words, k_scales, vT, vs, offs, out):
                 ks_pool[r:P:32, :, :].bitcast(I32),
                 k_scales[:, r:16:4, :].rearrange("o quad t -> quad o t").bitcast(I32),
             )
-        nc.scalar.copy(one[:], one_set[:])
         nc.sync.dma_start(q_raw[:], qT[0].rearrange("(o p j) q -> p o j q", p=P, j=PACK))
         nc.sync.dma_start(v_pool[0][:], vT[0:P, :])
 
@@ -78,23 +78,28 @@ def tile_attend_relu2_srt_kernel(tc, qT, k_words, k_scales, vT, vs, offs, out):
         for o in range(PASSES):
             nc.vector.tensor_copy(kw[o][:].bitcast(U16), halves[:, o, :])
 
-        q_bf = lay.tile([P, PASSES, NQ, PACK], BF16, name="q_bf", align_bytes=64, offset=20480)
-        nc.scalar.copy(q_bf[:], q_raw[:].rearrange("p o j q -> p o q j"))
-        q_codes = sb.tile([P, PASSES * NQ], U32, name="q_codes", align_bytes=64)
-        q_scales = sb.tile([P, PASSES * NQ], U8, name="q_scales", align_bytes=64)
-        nc.vector.quantize_mx(out=q_codes[:].bitcast(FP8X4), scales=q_scales[:], in_=q_bf[:].rearrange("p o q j -> p (o q j)"))
-
+        q_bf = [
+            lay.tile([P, NQ, PACK], BF16, name=f"q_bf{o}", align_bytes=64, offset=20480 + 1024 * o) for o in range(PASSES)
+        ]
+        q_codes = [sb.tile([P, NQ], U32, name=f"q_codes{o}", align_bytes=64) for o in range(PASSES)]
+        q_scales = [sb.tile([P, NQ], U8, name=f"q_scales{o}", align_bytes=64) for o in range(PASSES)]
+        for o in range(PASSES):
+            nc.scalar.copy(
+                q_bf[o][:].rearrange("p (c i) j -> p c j i", i=4),
+                q_raw[:, o, :, :].rearrange("p j (c i) -> p c j i", i=4),
+            )
+        nc.vector.quantize_mx(out=q_codes[0][:].bitcast(FP8X4), scales=q_scales[0][:], in_=q_bf[0][:].rearrange("p q j -> p (q j)"))
         ks1 = lay.tile([P, SLOTS], U8, name="ks1", align_bytes=64, offset=20480)
         nc.vector.tensor_copy(ks1[:], ks_pool[:, 1, :].indirect(offsets[:]))
+        nc.vector.quantize_mx(out=q_codes[1][:].bitcast(FP8X4), scales=q_scales[1][:], in_=q_bf[1][:].rearrange("p q j -> p (q j)"))
         ks = [ks0, ks1]
 
         scores = ps.tile([P, SLOTS], F32, name="scores")
         for o in range(PASSES):
-            cols = slice(o * NQ, (o + 1) * NQ)
             nc.tensor.matmul_mx(
                 out=scores[:],
-                lhsT=q_codes[:, cols].bitcast(FP8X4),
-                lhsT_scale=q_scales[:, cols],
+                lhsT=q_codes[o][:].bitcast(FP8X4),
+                lhsT_scale=q_scales[o][:],
                 rhs=kw[o][:].bitcast(FP4X4),
                 rhs_scale=ks[o][:],
                 start=(o == 0),
@@ -143,9 +148,9 @@ def tile_attend_relu2_srt_kernel(tc, qT, k_words, k_scales, vT, vs, offs, out):
         nc.scalar.activation(part[:], total[:, 0:1], ACT.Identity, bias=one[:, 0:1])
         nc.scalar.activation(denom[:], total[:, 1:2], ACT.Identity, bias=part[:])
         inv = lay.tile([P, 1], F32, name="inv", offset=12288 + 2048)
-        nc.vector.reciprocal(inv[:], denom[:])
 
         nc.vector.quantize_mx(out=v_codes[1][:].bitcast(FP8X4), scales=v_scales[1][:], in_=v_bf[1][:])
+        nc.vector.reciprocal(inv[:], denom[:])
 
         for j in range(PLANES):
             sums = ps.tile([P, P], F32, name=f"sums{j}")

from contextlib import ExitStack

import concourse.mybir as mybir
from concourse.masks import make_identity

F32 = mybir.dt.float32
BF16 = mybir.dt.bfloat16
I32 = mybir.dt.int32
U32 = mybir.dt.uint32
U16 = mybir.dt.uint16
U8 = mybir.dt.uint8
FP8X4 = mybir.dt.float8_e4m3fn_x4
FP4X4 = mybir.dt.float4_e2m1fn_x4
ACT = mybir.ActivationFunctionType
ALU = mybir.AluOpType

P = 128
PACK = 4
SLOTS, POOL, D, DV, NQ = 512, 2048, 1024, 256, 128
PASSES = D // (P * PACK)
PLANES = DV // P
VS_ROW = P - 1

FLOPS = 2 * NQ * SLOTS * (D + DV)
BYTES = 4 * D * NQ + 4 * P * POOL + 32 * POOL + 4 * DV * POOL + 4 * POOL + 2 * SLOTS + 4 * NQ * DV


def tile_attend_relu2_srt_kernel(tc, qT, k_words, k_scales, vT, vs, offs, out):
    nc = tc.nc
    with ExitStack() as ctx:
        sb = ctx.enter_context(tc.tile_pool(name="sb", bufs=1))
        lay = ctx.enter_context(tc.tile_pool(name="lay", bufs=1))
        ps = ctx.enter_context(tc.psum_pool(name="ps", bufs=1))

        offsets = sb.tile([P, SLOTS // 16], U16, name="offsets")
        kw_pool = sb.tile([P, POOL], I32, name="kw_pool")
        ks_pool = sb.tile([P, PASSES, POOL], U8, name="ks_pool")
        vs_pool = lay.tile([P, POOL], F32, name="vs_pool", offset=12288)
        one_set = lay.tile([P, 16], F32, name="one_set", offset=4096 - 32)
        q_raw = lay.tile([P, PASSES, PACK, NQ], F32, name="q_raw", offset=0)
        v_pool = [lay.tile([P, POOL], F32, name=f"v_pool{j}", offset=(4096, 12288)[j]) for j in range(PLANES)]
        one = sb.tile([P, 16], F32, name="one")
        ident = sb.tile([P, P], F32, name="ident")

        nc.vector.memset(ks_pool[:].rearrange("p o t -> p (o t)").bitcast(I32), 0)
        nc.vector.memset(one_set[:], 1.0)
        nc.vector.tensor_copy(one[:], one_set[:])
        nc.vector.memset(vs_pool[0:VS_ROW, POOL // 2 :].bitcast(I32), 0)
        nc.gpsimd.memset(vs_pool[0:VS_ROW, : POOL // 2].bitcast(I32), 0)
        make_identity(nc, ident[:])

        nc.sync.dma_start(offsets[:], offs)
        nc.scalar.dma_start(vs_pool[VS_ROW:P, :], vs[0:1, :])
        nc.sync.dma_start(kw_pool[:], k_words[0].rearrange("p t b -> p (t b)").bitcast(I32))
        for r in range(4):
            nc.sync.dma_start(
                ks_pool[r:P:32, :, :].bitcast(I32),
                k_scales[:, r:16:4, :].rearrange("o quad t -> quad o t").bitcast(I32),
            )
        nc.sync.dma_start(q_raw[:], qT[0].rearrange("(o p j) q -> p o j q", p=P, j=PACK))
        nc.sync.dma_start(v_pool[0][:], vT[0:P, :])

        vs_listed = sb.tile([P, SLOTS], F32, name="vs_listed")
        nc.vector.tensor_copy(vs_listed[:], vs_pool[:].indirect(offsets[:]))
        nc.sync.dma_start(v_pool[1][:], vT[P : 2 * P, :])
        vs_turned = ps.tile([P, PACK, P], F32, name="vs_turned")
        for t in range(PACK):
            nc.tensor.transpose(vs_turned[:, t, :], vs_listed[:, t:SLOTS:PACK], ident[:])
        vs_cols = sb.tile([P, PACK], F32, name="vs_cols")
        nc.scalar.copy(vs_cols[:], vs_turned[:, :, VS_ROW])

        kw_pairs = sb.tile([P, SLOTS], U32, name="kw_pairs")
        nc.vector.tensor_copy(kw_pairs[:], kw_pool[:].bitcast(U32).indirect(offsets[:]))
        ks0 = sb.tile([P, SLOTS], U8, name="ks0", align_bytes=64)
        nc.vector.tensor_copy(ks0[:], ks_pool[:, 0, :].indirect(offsets[:]))
        kw = [sb.tile([P, 2 * SLOTS], U8, name=f"kw{o}", align_bytes=64) for o in range(PASSES)]
        halves = kw_pairs[:].bitcast(U16).rearrange("p (s h) -> p h s", h=2)
        for o in range(PASSES):
            nc.vector.tensor_copy(kw[o][:].bitcast(U16), halves[:, o, :])

        q_bf = [
            lay.tile([P, NQ, PACK], BF16, name=f"q_bf{o}", align_bytes=64, offset=20480 + 1024 * o) for o in range(PASSES)
        ]
        q_codes = [sb.tile([P, NQ], U32, name=f"q_codes{o}", align_bytes=64) for o in range(PASSES)]
        q_scales = [sb.tile([P, NQ], U8, name=f"q_scales{o}", align_bytes=64) for o in range(PASSES)]
        for o in range(PASSES):
            nc.scalar.copy(
                q_bf[o][:].rearrange("p (c i) j -> p c j i", i=4),
                q_raw[:, o, :, :].rearrange("p j (c i) -> p c j i", i=4),
            )
        nc.vector.quantize_mx(out=q_codes[0][:].bitcast(FP8X4), scales=q_scales[0][:], in_=q_bf[0][:].rearrange("p q j -> p (q j)"))
        ks1 = lay.tile([P, SLOTS], U8, name="ks1", align_bytes=64, offset=20480)
        nc.vector.tensor_copy(ks1[:], ks_pool[:, 1, :].indirect(offsets[:]))
        nc.vector.quantize_mx(out=q_codes[1][:].bitcast(FP8X4), scales=q_scales[1][:], in_=q_bf[1][:].rearrange("p q j -> p (q j)"))
        ks = [ks0, ks1]

        scores = ps.tile([P, SLOTS], F32, name="scores")
        for o in range(PASSES):
            nc.tensor.matmul_mx(
                out=scores[:],
                lhsT=q_codes[o][:].bitcast(FP8X4),
                lhsT_scale=q_scales[o][:],
                rhs=kw[o][:].bitcast(FP4X4),
                rhs_scale=ks[o][:],
                start=(o == 0),
                stop=(o == PASSES - 1),
            )

        pos = sb.tile([P, PACK, P], F32, name="pos")
        prob = sb.tile([P, PACK, P], F32, name="prob")
        total = sb.tile([P, 2], F32, name="total")
        prob_turned = ps.tile([P, PACK, NQ], F32, name="prob_turned")
        dealt = scores[:].rearrange("q (s t) -> q t s", t=PACK)
        for half in range(2):
            places = slice(2 * half, 2 * half + 2)
            nc.scalar.activation(pos[:, places, :], dealt[:, places, :], ACT.Relu)
            nc.scalar.activation(prob[:, places, :], pos[:, places, :], ACT.Square, accum_out=total[:, half : half + 1])
            for t in range(2 * half, 2 * half + 2):
                nc.tensor.transpose(prob_turned[:, t, :], prob[:, t, :], ident[:])

        v_bf = []
        for j in range(PLANES):
            v_listed = lay.tile([P, SLOTS], BF16, name=f"v_listed{j}", offset=(21504, 22528)[j])
            nc.vector.tensor_copy(v_listed[:], v_pool[j][:].indirect(offsets[:]))
            v_words = v_listed[:].bitcast(F32)
            v_turned = ps.tile([P, 2, P], F32, name=f"v_turned{j}")
            for u in range(2):
                nc.tensor.transpose(v_turned[:, u, :], v_words[:, u : SLOTS // 2 : 2], ident[:])
            v_bf.append(sb.tile([P, P * PACK], BF16, name=f"v_bf{j}", align_bytes=64))
            nc.scalar.copy(v_bf[j][:].bitcast(F32).rearrange("p (e u) -> p e u", u=2), v_turned[:].rearrange("p u e -> p e u"))

        w_bf = lay.tile([P, NQ, PACK], BF16, name="w_bf", align_bytes=64, offset=12288)
        nc.vector.tensor_tensor(
            w_bf[:],
            prob_turned[:].rearrange("p t q -> p q t"),
            vs_cols[:].unsqueeze(1).to_broadcast([P, NQ, PACK]),
            ALU.mult,
        )
        v_codes = [lay.tile([P, P], U32, name=f"v_codes{j}", align_bytes=64, offset=12288 + 1024 + 512 * j) for j in range(PLANES)]
        v_scales = [sb.tile([P, P], U8, name=f"v_scales{j}", align_bytes=64) for j in range(PLANES)]
        nc.vector.quantize_mx(out=v_codes[0][:].bitcast(FP8X4), scales=v_scales[0][:], in_=v_bf[0][:])
        w_codes = sb.tile([P, NQ], U32, name="w_codes", align_bytes=64)
        w_scales = sb.tile([P, NQ], U8, name="w_scales", align_bytes=64)
        nc.vector.quantize_mx(out=w_codes[:].bitcast(FP8X4), scales=w_scales[:], in_=w_bf[:].rearrange("p q t -> p (q t)"))

        denom = sb.tile([P, 1], F32, name="denom")
        part = sb.tile([P, 1], F32, name="part")
        nc.scalar.activation(part[:], total[:, 0:1], ACT.Identity, bias=one[:, 0:1])
        nc.scalar.activation(denom[:], total[:, 1:2], ACT.Identity, bias=part[:])
        inv = lay.tile([P, 1], F32, name="inv", offset=12288 + 2048)

        nc.vector.quantize_mx(out=v_codes[1][:].bitcast(FP8X4), scales=v_scales[1][:], in_=v_bf[1][:])
        nc.vector.reciprocal(inv[:], denom[:])

        for j in range(PLANES):
            sums = ps.tile([P, P], F32, name=f"sums{j}")
            nc.tensor.matmul_mx(
                out=sums[:],
                lhsT=w_codes[:].bitcast(FP8X4),
                lhsT_scale=w_scales[:],
                rhs=v_codes[j][:].bitcast(FP8X4),
                rhs_scale=v_scales[j][:],
                start=True,
                stop=True,
            )
            y = sb.tile([P, P], F32, name=f"y{j}")
            nc.scalar.activation(y[:], sums[:], ACT.Copy, scale=inv[:])
            nc.sync.dma_start(out[0][:, j * P : (j + 1) * P], y[:])
